import numpy as np
import ml_dtypes


def mxq(x, axis, fmt="e4m3"):
    dtype, down = {"e4m3": (ml_dtypes.float8_e4m3fn, 7), "e5m2": (ml_dtypes.float8_e5m2, 14)}[fmt]
    v = np.moveaxis(np.asarray(x, np.float32).astype(ml_dtypes.bfloat16).astype(np.float64), axis, -1)
    blocks = v.reshape(v.shape[:-1] + (-1, 32))
    amax = np.abs(blocks).max(-1, keepdims=True)
    byte = np.maximum(np.where(amax > 0, np.frexp(amax)[1] - 1 + 127, 0) - down, 1)
    scale = np.exp2(byte - 127.0)
    codes = (blocks / scale).astype(np.float32).astype(dtype).astype(np.float64)
    return np.moveaxis((codes * scale).reshape(v.shape), -1, axis)


WIDE = False


def mx_kscale(k):
    if not WIDE:
        return np.ones(k)
    levels = np.array([10, -10, 5, -5, 0])
    if k % 512:
        return np.exp2(np.random.permutation(np.resize(levels, k // 32))).repeat(32)
    a = np.empty((k // 512, 16))
    for p in range(k // 512):
        a[p, :8] = np.random.permutation(np.resize(levels, 8))
        for g in range(8):
            far = levels[np.abs(levels - a[p, g]) >= 10]
            a[p, g + 8] = far[np.random.randint(len(far))]
    return np.exp2(a.ravel()).repeat(32)


def f64(x):
    return np.asarray(x).astype(np.float64)


def striped8(idx):
    return np.asarray(idx).reshape(8, -1, 16).transpose(0, 2, 1).reshape(128, -1).astype(np.uint16)


def unstriped8(offs):
    return offs.reshape(8, 16, -1).transpose(0, 2, 1).reshape(8, -1).astype(np.int64)


def pick8(x, idx, run):
    r = np.arange(len(x))
    return x[r[:, None], idx[r % (8 * run) // run]]


E2M1 = np.array([0.0, 0.5, 1.0, 1.5, 2.0, 3.0, 4.0, 6.0, -0.0, -0.5, -1.0, -1.5, -2.0, -3.0, -4.0, -6.0])


def pack_weight(w, fmt):
    k, n = w.shape
    w = f64(np.asarray(w, np.float32).astype(ml_dtypes.bfloat16)).reshape(k // 32, 32, n)
    amax = np.abs(w).max(1)
    if fmt == "e4m3":
        byte = np.frexp(amax)[1] - 1 + 127 - 7
    else:
        mant, ex = np.frexp(amax / 6.0)
        byte = np.where(mant > 0.5, ex, ex - 1) + 127
    byte = np.clip(np.where(amax > 0, byte, 1), 1, 254)
    scaled = (w * np.exp2(127.0 - byte)[:, None, :]).reshape(k, n).astype(np.float32)
    by_word = np.ascontiguousarray(scaled.reshape(k // 512, 128, 4, n).transpose(0, 1, 3, 2))
    if fmt == "e4m3":
        words = by_word.astype(ml_dtypes.float8_e4m3fn).view(np.uint8)
    else:
        c = by_word.astype(ml_dtypes.float4_e2m1fn).view(np.uint8) & 0xF
        words = (c[..., 0::2] | (c[..., 1::2] << 4)).reshape(k // 512, 128, 2 * n)
    return np.ascontiguousarray(words), np.ascontiguousarray(byte.astype(np.uint8).reshape(k // 512, 16, n))


def unpack_weight(words, scales, fmt):
    g, _, n = scales.shape
    words = np.ascontiguousarray(words).reshape(g, 128, n, -1)
    if fmt == "e4m3":
        vals = words.view(ml_dtypes.float8_e4m3fn).astype(np.float64)
    else:
        nib = np.empty((g, 128, n, 4), np.uint8)
        nib[..., 0::2] = words & 0xF
        nib[..., 1::2] = words >> 4
        vals = E2M1[nib]
    vals = vals * np.repeat(np.exp2(scales.astype(np.float64) - 127.0), 8, axis=1)[..., None]
    return vals.transpose(0, 1, 3, 2).reshape(g * 512, n)


D, T, U, X, I, Q = 512, 1024, 1024, 1024, 512, 128


def setup_inputs():
    n = np.random.standard_normal
    idx = np.stack([np.random.permutation(T)[:I] for _ in range(8)])
    idx2 = np.stack([np.random.permutation(X)[:I] for _ in range(8)])
    idx3 = np.stack([np.random.permutation(X)[:I] for _ in range(8)])
    idx4 = np.stack([np.random.permutation(U)[:I] for _ in range(8)])
    idx5 = np.stack([np.random.permutation(U)[:I] for _ in range(8)])
    idx6 = np.stack([np.random.permutation(U)[:I] for _ in range(8)])
    fd = mx_kscale(D)
    keysp = pack_weight(n((D, T)) / fd[:, None], "e2m1")
    notesp = pack_weight(n((D, U)) / fd[:, None], "e4m3")
    usersp = pack_weight(n((D, X)) / fd[:, None], "e2m1")
    return {
        "query": (n((D, Q)) * 1.0 / np.sqrt(D) * fd[:, None]).astype(np.float32),
        "keys_words": keysp[0],
        "keys_scales": keysp[1],
        "notes_words": notesp[0],
        "notes_scales": notesp[1],
        "users_words": usersp[0],
        "users_scales": usersp[1],
        "offs": striped8(idx),
        "offs2": striped8(idx2),
        "offs3": striped8(idx3),
        "offs4": striped8(idx4),
        "offs5": striped8(idx5),
        "offs6": striped8(idx6),
    }


def reference(query, keys_words, keys_scales, notes_words, notes_scales, users_words, users_scales, offs, offs2, offs3, offs4, offs5, offs6):
    idx = unstriped8(offs)
    idx2 = unstriped8(offs2)
    idx3 = unstriped8(offs3)
    idx4 = unstriped8(offs4)
    idx5 = unstriped8(offs5)
    idx6 = unstriped8(offs6)
    keysu = unpack_weight(keys_words, keys_scales, "e2m1")
    notesu = unpack_weight(notes_words, notes_scales, "e4m3")
    usersu = unpack_weight(users_words, users_scales, "e2m1")
    queryq = mxq(f64(query), 0, "e4m3")
    a = queryq.T @ keysu
    b = queryq.T @ notesu
    c0 = queryq.T @ usersu
    ta = np.max(a, axis=1, keepdims=True)
    e1 = np.exp(pick8(a, idx, 16) - ta)
    f1 = np.zeros((Q, X))
    f1[np.arange(Q)[:, None], idx2[np.arange(Q) % 128 // 16]] = e1
    cc = c0 + f1 * 4.0
    w = pick8(cc, idx3, 16) - pick8(b, idx4, 16)
    f2 = np.zeros((Q, U))
    f2[np.arange(Q)[:, None], idx5[np.arange(Q) % 128 // 16]] = w
    bb = b + f2
    y = pick8(bb, idx6, 16)
    return y

@@ -1,0 +1,136 @@
+from contextlib import ExitStack
+
+import concourse.mybir as mybir
+
+D, T, U, X, I, Q = 512, 1024, 1024, 1024, 512, 128
+FLOPS = 2 * D * Q * (T + U + X)
+
+F32 = mybir.dt.float32
+BF16 = mybir.dt.bfloat16
+I32 = mybir.dt.int32
+U32 = mybir.dt.uint32
+U16 = mybir.dt.uint16
+U8 = mybir.dt.uint8
+FP8X4 = mybir.dt.float8_e4m3fn_x4
+FP4X4 = mybir.dt.float4_e2m1fn_x4
+ALU = mybir.AluOpType
+ACT = mybir.ActivationFunctionType
+
+P = 128
+PACK = 4
+BANK = 512
+A_CHUNK = 256
+HALF = I // 2
+GROUP = 16
+
+
+def load_scales(nc, plane, scales):
+    for r in range(4):
+        nc.sync.dma_start(out=plane[r:P:32, :].bitcast(I32), in_=scales[0, r:16:4, :].bitcast(I32))
+
+
+def tile_attend_courier_three_kernel(tc, query, keys_words, keys_scales, notes_words, notes_scales,
+                                      users_words, users_scales, offs, offs2, offs3, offs4, offs5, offs6, out):
+    nc = tc.nc
+    with ExitStack() as ctx:
+        keep = ctx.enter_context(tc.tile_pool(name="keep", bufs=1))
+        psum = ctx.enter_context(tc.psum_pool(name="psum", bufs=1))
+
+        def list_tile(name):
+            return keep.tile([P, I // GROUP], U16, name=name)
+
+        def half(lists, h):
+            return lists[:, h * HALF // GROUP:(h + 1) * HALF // GROUP]
+
+        l1, l2, l3, l4, l5, l6 = [list_tile("list%d" % n) for n in range(1, 7)]
+        q_raw = keep.tile([P, PACK, Q], F32)
+        k_words = keep.tile([P, 2 * T], U8, align_bytes=64)
+        k_plane = keep.tile([P, T], U8, align_bytes=64)
+        n_words = keep.tile([P, U], U32, align_bytes=64)
+        n_plane = keep.tile([P, U], U8, align_bytes=64)
+        u_words = keep.tile([P, 2 * X], U8, align_bytes=64)
+        u_plane = keep.tile([P, X], U8, align_bytes=64)
+        f1 = keep.tile([P, X], F32)
+        f2 = keep.tile([P, U], F32)
+
+        nc.vector.memset(k_plane[:].bitcast(I32), 0)
+        nc.vector.memset(n_plane[:].bitcast(I32), 0)
+        nc.vector.memset(u_plane[:].bitcast(I32), 0)
+        nc.vector.memset(f1[:], 0.0)
+
+        nc.sync.dma_start(out=q_raw[:], in_=query.rearrange("(p j) q -> p j q", j=PACK))
+        nc.sync.dma_start(out=k_words[:].bitcast(I32), in_=keys_words[0].bitcast(I32))
+        load_scales(nc, k_plane, keys_scales)
+        nc.sync.dma_start(l1[:], offs)
+        nc.sync.dma_start(l2[:], offs2)
+        nc.sync.dma_start(out=n_words[:].bitcast(I32),
+                          in_=notes_words[0].rearrange("p n t -> p (n t)").bitcast(I32))
+        load_scales(nc, n_plane, notes_scales)
+        nc.sync.dma_start(l4[:], offs4)
+        nc.sync.dma_start(out=u_words[:].bitcast(I32), in_=users_words[0].bitcast(I32))
+        load_scales(nc, u_plane, users_scales)
+        nc.sync.dma_start(l3[:], offs3)
+        nc.sync.dma_start(l5[:], offs5)
+        nc.sync.dma_start(l6[:], offs6)
+
+        q_bf = keep.tile([P, Q, PACK], BF16, align_bytes=64)
+        nc.vector.tensor_copy(out=q_bf[:], in_=q_raw[:].rearrange("p j q -> p q j"))
+        q_codes = keep.tile([P, Q], U32, align_bytes=64)
+        q_plane = keep.tile([P, Q], U8, align_bytes=64)
+        nc.vector.quantize_mx(out=q_codes[:].bitcast(FP8X4), scales=q_plane[:],
+                              in_=q_bf[:].rearrange("p q j -> p (q j)"))
+
+        def scores(name, words, plane, width):
+            bank = psum.tile([P, width], F32, name=name)
+            nc.tensor.matmul_mx(out=bank[:], lhsT=q_codes[:].bitcast(FP8X4), lhsT_scale=q_plane[:],
+                                rhs=words, rhs_scale=plane, start=True, stop=True)
+            return bank
+
+        a = keep.tile([P, T], F32)
+        chunks = T // A_CHUNK
+        a_max = keep.tile([P, chunks], F32)
+        for c in range(chunks):
+            c0, c1 = c * A_CHUNK, (c + 1) * A_CHUNK
+            bank = scores("a%d" % c, k_words[:, 2 * c0:2 * c1].bitcast(FP4X4), k_plane[:, c0:c1], A_CHUNK)
+            nc.vector.tensor_scalar(out=a[:, c0:c1], in0=bank[:], scalar1=1.0, scalar2=None,
+                                    op0=ALU.mult, op1=ALU.max, accum_out=a_max[:, c:c + 1])
+        neg_ta = keep.tile([P, 1], F32)
+        nc.vector.tensor_reduce(out=neg_ta[:], in_=a_max[:], axis=mybir.AxisListType.X, op=ALU.max, negate=True)
+
+        nc.vector.memset(f2[:], 0.0)
+        for h in range(2):
+            e1 = keep.tile([P, HALF], F32, name="e1_%d" % h)
+            nc.scalar.activation(out=e1[:], in_=a[:].indirect(half(l1, h)), func=ACT.Exp, bias=neg_ta[:])
+            nc.vector.tensor_copy(out=f1[:].indirect(half(l2, h)), in_=e1[:])
+
+        b = keep.tile([P, U], F32)
+        for c in range(U // BANK):
+            c0, c1 = c * BANK, (c + 1) * BANK
+            bank = scores("b%d" % c, n_words[:, c0:c1].bitcast(FP8X4), n_plane[:, c0:c1], BANK)
+            nc.scalar.copy(out=b[:, c0:c1], in_=bank[:])
+        neg_b = keep.tile([P, I], F32)
+        nc.scalar.activation(out=neg_b[:], in_=b[:].indirect(l4[:]), func=ACT.Copy, scale=-1.0)
+
+        cc = keep.tile([P, X], F32)
+        for c in range(X // BANK):
+            c0, c1 = c * BANK, (c + 1) * BANK
+            bank = scores("c%d" % c, u_words[:, 2 * c0:2 * c1].bitcast(FP4X4), u_plane[:, c0:c1], BANK)
+            nc.vector.scalar_tensor_tensor(out=cc[:, c0:c1], in0=f1[:, c0:c1], scalar=4.0, in1=bank[:],
+                                           op0=ALU.mult, op1=ALU.add)
+
+        cc_lo = keep.tile([P, HALF], F32)
+        cc_hi = keep.tile([P, HALF], F32)
+        nc.vector.tensor_copy(out=cc_lo[:], in_=cc[:].indirect(half(l3, 0)))
+        nc.scalar.activation(out=cc_hi[:], in_=cc[:].indirect(half(l3, 1)), func=ACT.Copy)
+        for h, picked in enumerate((cc_lo, cc_hi)):
+            nc.vector.tensor_tensor(out=f2[:].indirect(half(l5, h)), in0=picked[:],
+                                    in1=neg_b[:, h * HALF:(h + 1) * HALF], op=ALU.add)
+
+        bb = keep.tile([P, U], F32)
+        nc.vector.tensor_tensor(out=bb[:], in0=b[:], in1=f2[:], op=ALU.add)
+        y_lo = keep.tile([P, HALF], F32)
+        y_hi = keep.tile([P, HALF], F32)
+        nc.vector.tensor_copy(out=y_lo[:], in_=bb[:].indirect(half(l6, 0)))
+        nc.scalar.activation(out=y_hi[:], in_=bb[:].indirect(half(l6, 1)), func=ACT.Copy)
+        nc.sync.dma_start(out=out[:, 0:HALF], in_=y_lo[:])
+        nc.scalar.dma_start(out=out[:, HALF:I], in_=y_hi[:])

@@ -22,6 +22,7 @@ BANK = 512
 A_CHUNK = 256
 HALF = I // 2
 GROUP = 16
+SPLIT = 704
 
 
 def load_scales(nc, plane, scales):
@@ -51,17 +52,18 @@ def tile_attend_courier_three_kernel(tc, query, keys_words, keys_scales, notes_w
         u_words = keep.tile([P, 2 * X], U8, align_bytes=64)
         u_plane = keep.tile([P, X], U8, align_bytes=64)
         f1 = keep.tile([P, X], F32)
-        f2 = keep.tile([P, U], F32)
 
         nc.vector.memset(k_plane[:].bitcast(I32), 0)
         nc.vector.memset(n_plane[:].bitcast(I32), 0)
         nc.vector.memset(u_plane[:].bitcast(I32), 0)
         nc.vector.memset(f1[:], 0.0)
+        fours = keep.tile([P, HALF], F32)
+        nc.vector.memset(fours[:], 4.0)
 
         nc.sync.dma_start(out=q_raw[:], in_=query.rearrange("(p j) q -> p j q", j=PACK))
+        nc.sync.dma_start(l1[:], offs)
         nc.sync.dma_start(out=k_words[:].bitcast(I32), in_=keys_words[0].bitcast(I32))
         load_scales(nc, k_plane, keys_scales)
-        nc.sync.dma_start(l1[:], offs)
         nc.sync.dma_start(l2[:], offs2)
         nc.sync.dma_start(out=n_words[:].bitcast(I32),
                           in_=notes_words[0].rearrange("p n t -> p (n t)").bitcast(I32))
@@ -88,7 +90,7 @@ def tile_attend_courier_three_kernel(tc, query, keys_words, keys_scales, notes_w
 
         a = keep.tile([P, T], F32)
         chunks = T // A_CHUNK
-        a_max = keep.tile([P, chunks], F32)
+        a_max = keep.tile([P, chunks], F32, tag="max_then_f2")
         for c in range(chunks):
             c0, c1 = c * A_CHUNK, (c + 1) * A_CHUNK
             bank = scores("a%d" % c, k_words[:, 2 * c0:2 * c1].bitcast(FP4X4), k_plane[:, c0:c1], A_CHUNK)
@@ -97,37 +99,43 @@ def tile_attend_courier_three_kernel(tc, query, keys_words, keys_scales, notes_w
         neg_ta = keep.tile([P, 1], F32)
         nc.vector.tensor_reduce(out=neg_ta[:], in_=a_max[:], axis=mybir.AxisListType.X, op=ALU.max, negate=True)
 
+        f2 = keep.tile([P, U], F32, tag="max_then_f2")
         nc.vector.memset(f2[:], 0.0)
         for h in range(2):
             e1 = keep.tile([P, HALF], F32, name="e1_%d" % h)
             nc.scalar.activation(out=e1[:], in_=a[:].indirect(half(l1, h)), func=ACT.Exp, bias=neg_ta[:])
-            nc.vector.tensor_copy(out=f1[:].indirect(half(l2, h)), in_=e1[:])
+            nc.vector.tensor_tensor(out=f1[:].indirect(half(l2, h)), in0=e1[:], in1=fours[:], op=ALU.mult)
+
+        def add_split(total, scattered, banks, tail):
+            nc.gpsimd.tensor_tensor(out=total[:, SPLIT:], in0=scattered[:, SPLIT:], in1=tail, op=ALU.add)
+            nc.vector.tensor_tensor(out=total[:, 0:BANK], in0=scattered[:, 0:BANK], in1=banks[0][:], op=ALU.add)
+            nc.vector.tensor_tensor(out=total[:, BANK:SPLIT], in0=scattered[:, BANK:SPLIT],
+                                    in1=banks[1][:, 0:SPLIT - BANK], op=ALU.add)
 
         b = keep.tile([P, U], F32)
+        b_banks = []
         for c in range(U // BANK):
             c0, c1 = c * BANK, (c + 1) * BANK
             bank = scores("b%d" % c, n_words[:, c0:c1].bitcast(FP8X4), n_plane[:, c0:c1], BANK)
             nc.scalar.copy(out=b[:, c0:c1], in_=bank[:])
+            b_banks.append(bank)
         neg_b = keep.tile([P, I], F32)
         nc.scalar.activation(out=neg_b[:], in_=b[:].indirect(l4[:]), func=ACT.Copy, scale=-1.0)
 
         cc = keep.tile([P, X], F32)
-        for c in range(X // BANK):
-            c0, c1 = c * BANK, (c + 1) * BANK
-            bank = scores("c%d" % c, u_words[:, 2 * c0:2 * c1].bitcast(FP4X4), u_plane[:, c0:c1], BANK)
-            nc.vector.scalar_tensor_tensor(out=cc[:, c0:c1], in0=f1[:, c0:c1], scalar=4.0, in1=bank[:],
-                                           op0=ALU.mult, op1=ALU.add)
+        c_banks = [scores("c%d" % c, u_words[:, 2 * c * BANK:2 * (c + 1) * BANK].bitcast(FP4X4),
+                          u_plane[:, c * BANK:(c + 1) * BANK], BANK) for c in range(X // BANK)]
+        c_tail = keep.tile([P, X - SPLIT], F32)
+        nc.scalar.copy(out=c_tail[:], in_=c_banks[1][:, SPLIT - BANK:])
+        add_split(cc, f1, c_banks, c_tail[:])
 
-        cc_lo = keep.tile([P, HALF], F32)
-        cc_hi = keep.tile([P, HALF], F32)
-        nc.vector.tensor_copy(out=cc_lo[:], in_=cc[:].indirect(half(l3, 0)))
-        nc.scalar.activation(out=cc_hi[:], in_=cc[:].indirect(half(l3, 1)), func=ACT.Copy)
-        for h, picked in enumerate((cc_lo, cc_hi)):
-            nc.vector.tensor_tensor(out=f2[:].indirect(half(l5, h)), in0=picked[:],
-                                    in1=neg_b[:, h * HALF:(h + 1) * HALF], op=ALU.add)
+        picked = keep.tile([P, I], F32)
+        nc.vector.tensor_copy(out=picked[:, 0:HALF], in_=cc[:].indirect(half(l3, 0)))
+        nc.scalar.activation(out=picked[:, HALF:I], in_=cc[:].indirect(half(l3, 1)), func=ACT.Copy)
+        nc.vector.tensor_tensor(out=f2[:].indirect(l5[:]), in0=picked[:], in1=neg_b[:], op=ALU.add)
 
         bb = keep.tile([P, U], F32)
-        nc.vector.tensor_tensor(out=bb[:], in0=b[:], in1=f2[:], op=ALU.add)
+        add_split(bb, f2, b_banks, b[:, SPLIT:])
         y_lo = keep.tile([P, HALF], F32)
         y_hi = keep.tile([P, HALF], F32)
         nc.vector.tensor_copy(out=y_lo[:], in_=bb[:].indirect(half(l6, 0)))

@@ -22,12 +22,12 @@ BANK = 512
 A_CHUNK = 256
 HALF = I // 2
 GROUP = 16
-SPLIT = 704
+SPLIT = 688
 
 
-def load_scales(nc, plane, scales):
-    for r in range(4):
-        nc.sync.dma_start(out=plane[r:P:32, :].bitcast(I32), in_=scales[0, r:16:4, :].bitcast(I32))
+def load_scales(queues, plane, scales):
+    for r, queue in enumerate(queues):
+        queue.dma_start(out=plane[r:P:32, :].bitcast(I32), in_=scales[0, r:16:4, :].bitcast(I32))
 
 
 def tile_attend_courier_three_kernel(tc, query, keys_words, keys_scales, notes_words, notes_scales,
@@ -45,7 +45,7 @@ def tile_attend_courier_three_kernel(tc, query, keys_words, keys_scales, notes_w
 
         l1, l2, l3, l4, l5, l6 = [list_tile("list%d" % n) for n in range(1, 7)]
         q_raw = keep.tile([P, PACK, Q], F32)
-        k_words = keep.tile([P, 2 * T], U8, align_bytes=64)
+        k_words = [keep.tile([P, 2 * BANK], U8, align_bytes=64, name="k_words%d" % c) for c in range(T // BANK)]
         k_plane = keep.tile([P, T], U8, align_bytes=64)
         n_words = keep.tile([P, U], U32, align_bytes=64)
         n_plane = keep.tile([P, U], U8, align_bytes=64)
@@ -62,15 +62,17 @@ def tile_attend_courier_three_kernel(tc, query, keys_words, keys_scales, notes_w
 
         nc.sync.dma_start(out=q_raw[:], in_=query.rearrange("(p j) q -> p j q", j=PACK))
         nc.sync.dma_start(l1[:], offs)
-        nc.sync.dma_start(out=k_words[:].bitcast(I32), in_=keys_words[0].bitcast(I32))
-        load_scales(nc, k_plane, keys_scales)
-        nc.sync.dma_start(l2[:], offs2)
+        load_scales([nc.scalar, nc.scalar, nc.sync, nc.sync], k_plane, keys_scales)
+        for c, words in enumerate(k_words):
+            nc.sync.dma_start(out=words[:].bitcast(I32),
+                              in_=keys_words[0, :, 2 * c * BANK:2 * (c + 1) * BANK].bitcast(I32))
         nc.sync.dma_start(out=n_words[:].bitcast(I32),
                           in_=notes_words[0].rearrange("p n t -> p (n t)").bitcast(I32))
-        load_scales(nc, n_plane, notes_scales)
-        nc.sync.dma_start(l4[:], offs4)
+        load_scales([nc.sync] * 4, n_plane, notes_scales)
+        nc.sync.dma_start(l2[:], offs2)
         nc.sync.dma_start(out=u_words[:].bitcast(I32), in_=users_words[0].bitcast(I32))
-        load_scales(nc, u_plane, users_scales)
+        load_scales([nc.sync] * 4, u_plane, users_scales)
+        nc.sync.dma_start(l4[:], offs4)
         nc.sync.dma_start(l3[:], offs3)
         nc.sync.dma_start(l5[:], offs5)
         nc.sync.dma_start(l6[:], offs6)
@@ -88,15 +90,15 @@ def tile_attend_courier_three_kernel(tc, query, keys_words, keys_scales, notes_w
                                 rhs=words, rhs_scale=plane, start=True, stop=True)
             return bank
 
-        a = keep.tile([P, T], F32)
+        a = keep.tile([P, T], F32, tag="a_then_tail")
         chunks = T // A_CHUNK
         a_max = keep.tile([P, chunks], F32, tag="max_then_f2")
         for c in range(chunks):
             c0, c1 = c * A_CHUNK, (c + 1) * A_CHUNK
-            bank = scores("a%d" % c, k_words[:, 2 * c0:2 * c1].bitcast(FP4X4), k_plane[:, c0:c1], A_CHUNK)
+            bank = scores("a%d" % c, k_words[c0 // BANK][:, 2 * (c0 % BANK):2 * (c0 % BANK + A_CHUNK)].bitcast(FP4X4), k_plane[:, c0:c1], A_CHUNK)
             nc.vector.tensor_scalar(out=a[:, c0:c1], in0=bank[:], scalar1=1.0, scalar2=None,
                                     op0=ALU.mult, op1=ALU.max, accum_out=a_max[:, c:c + 1])
-        neg_ta = keep.tile([P, 1], F32)
+        neg_ta = keep.tile([P, 1], F32, tag="bias_then_b")
         nc.vector.tensor_reduce(out=neg_ta[:], in_=a_max[:], axis=mybir.AxisListType.X, op=ALU.max, negate=True)
 
         f2 = keep.tile([P, U], F32, tag="max_then_f2")
@@ -112,7 +114,7 @@ def tile_attend_courier_three_kernel(tc, query, keys_words, keys_scales, notes_w
             nc.vector.tensor_tensor(out=total[:, BANK:SPLIT], in0=scattered[:, BANK:SPLIT],
                                     in1=banks[1][:, 0:SPLIT - BANK], op=ALU.add)
 
-        b = keep.tile([P, U], F32)
+        b = keep.tile([P, U], F32, tag="bias_then_b")
         b_banks = []
         for c in range(U // BANK):
             c0, c1 = c * BANK, (c + 1) * BANK
@@ -125,8 +127,9 @@ def tile_attend_courier_three_kernel(tc, query, keys_words, keys_scales, notes_w
         cc = keep.tile([P, X], F32)
         c_banks = [scores("c%d" % c, u_words[:, 2 * c * BANK:2 * (c + 1) * BANK].bitcast(FP4X4),
                           u_plane[:, c * BANK:(c + 1) * BANK], BANK) for c in range(X // BANK)]
-        c_tail = keep.tile([P, X - SPLIT], F32)
+        c_tail = keep.tile([P, X - SPLIT], F32, tag="a_then_tail")
         nc.scalar.copy(out=c_tail[:], in_=c_banks[1][:, SPLIT - BANK:])
+
         add_split(cc, f1, c_banks, c_tail[:])
 
         picked = keep.tile([P, I], F32)
@@ -136,9 +139,7 @@ def tile_attend_courier_three_kernel(tc, query, keys_words, keys_scales, notes_w
 
         bb = keep.tile([P, U], F32)
         add_split(bb, f2, b_banks, b[:, SPLIT:])
-        y_lo = keep.tile([P, HALF], F32)
-        y_hi = keep.tile([P, HALF], F32)
-        nc.vector.tensor_copy(out=y_lo[:], in_=bb[:].indirect(half(l6, 0)))
-        nc.scalar.activation(out=y_hi[:], in_=bb[:].indirect(half(l6, 1)), func=ACT.Copy)
-        nc.sync.dma_start(out=out[:, 0:HALF], in_=y_lo[:])
-        nc.scalar.dma_start(out=out[:, HALF:I], in_=y_hi[:])
+        y = keep.tile([P, I], F32)
+        nc.vector.tensor_copy(out=y[:, 0:HALF], in_=bb[:].indirect(half(l6, 0)))
+        nc.scalar.activation(out=y[:, HALF:I], in_=bb[:].indirect(half(l6, 1)), func=ACT.Copy)
+        nc.sync.dma_start(out=out, in_=y[:])

@@ -66,13 +66,13 @@ def tile_attend_courier_three_kernel(tc, query, keys_words, keys_scales, notes_w
         for c, words in enumerate(k_words):
             nc.sync.dma_start(out=words[:].bitcast(I32),
                               in_=keys_words[0, :, 2 * c * BANK:2 * (c + 1) * BANK].bitcast(I32))
+        nc.sync.dma_start(l2[:], offs2)
+        load_scales([nc.sync] * 4, n_plane, notes_scales)
         nc.sync.dma_start(out=n_words[:].bitcast(I32),
                           in_=notes_words[0].rearrange("p n t -> p (n t)").bitcast(I32))
-        load_scales([nc.sync] * 4, n_plane, notes_scales)
-        nc.sync.dma_start(l2[:], offs2)
         nc.sync.dma_start(out=u_words[:].bitcast(I32), in_=users_words[0].bitcast(I32))
-        load_scales([nc.sync] * 4, u_plane, users_scales)
         nc.sync.dma_start(l4[:], offs4)
+        load_scales([nc.sync] * 4, u_plane, users_scales)
         nc.sync.dma_start(l3[:], offs3)
         nc.sync.dma_start(l5[:], offs5)
         nc.sync.dma_start(l6[:], offs6)

@@ -78,7 +78,8 @@ def tile_attend_courier_three_kernel(tc, query, keys_words, keys_scales, notes_w
         nc.sync.dma_start(l6[:], offs6)
 
         q_bf = keep.tile([P, Q, PACK], BF16, align_bytes=64)
-        nc.vector.tensor_copy(out=q_bf[:], in_=q_raw[:].rearrange("p j q -> p q j"))
+        nc.vector.tensor_copy(out=q_bf[:].rearrange("p (c i) j -> p c j i", i=4),
+                              in_=q_raw[:].rearrange("p j (c i) -> p c j i", i=4))
         q_codes = keep.tile([P, Q], U32, align_bytes=64)
         q_plane = keep.tile([P, Q], U8, align_bytes=64)
         nc.vector.quantize_mx(out=q_codes[:].bitcast(FP8X4), scales=q_plane[:],

from contextlib import ExitStack

import concourse.mybir as mybir

D, T, U, X, I, Q = 512, 1024, 1024, 1024, 512, 128
FLOPS = 2 * D * Q * (T + U + X)

F32 = mybir.dt.float32
BF16 = mybir.dt.bfloat16
I32 = mybir.dt.int32
U32 = mybir.dt.uint32
U16 = mybir.dt.uint16
U8 = mybir.dt.uint8
FP8X4 = mybir.dt.float8_e4m3fn_x4
FP4X4 = mybir.dt.float4_e2m1fn_x4
ALU = mybir.AluOpType
ACT = mybir.ActivationFunctionType

P = 128
PACK = 4
BANK = 512
A_CHUNK = 256
HALF = I // 2
GROUP = 16
SPLIT = 688


def load_scales(queues, plane, scales):
    for r, queue in enumerate(queues):
        queue.dma_start(out=plane[r:P:32, :].bitcast(I32), in_=scales[0, r:16:4, :].bitcast(I32))


def tile_attend_courier_three_kernel(tc, query, keys_words, keys_scales, notes_words, notes_scales,
                                      users_words, users_scales, offs, offs2, offs3, offs4, offs5, offs6, out):
    nc = tc.nc
    with ExitStack() as ctx:
        keep = ctx.enter_context(tc.tile_pool(name="keep", bufs=1))
        psum = ctx.enter_context(tc.psum_pool(name="psum", bufs=1))

        def list_tile(name):
            return keep.tile([P, I // GROUP], U16, name=name)

        def half(lists, h):
            return lists[:, h * HALF // GROUP:(h + 1) * HALF // GROUP]

        l1, l2, l3, l4, l5, l6 = [list_tile("list%d" % n) for n in range(1, 7)]
        q_raw = keep.tile([P, PACK, Q], F32)
        k_words = [keep.tile([P, 2 * BANK], U8, align_bytes=64, name="k_words%d" % c) for c in range(T // BANK)]
        k_plane = keep.tile([P, T], U8, align_bytes=64)
        n_words = keep.tile([P, U], U32, align_bytes=64)
        n_plane = keep.tile([P, U], U8, align_bytes=64)
        u_words = keep.tile([P, 2 * X], U8, align_bytes=64)
        u_plane = keep.tile([P, X], U8, align_bytes=64)
        f1 = keep.tile([P, X], F32)

        nc.vector.memset(k_plane[:].bitcast(I32), 0)
        nc.vector.memset(n_plane[:].bitcast(I32), 0)
        nc.vector.memset(u_plane[:].bitcast(I32), 0)
        nc.vector.memset(f1[:], 0.0)
        fours = keep.tile([P, HALF], F32)
        nc.vector.memset(fours[:], 4.0)

        nc.sync.dma_start(out=q_raw[:], in_=query.rearrange("(p j) q -> p j q", j=PACK))
        nc.sync.dma_start(l1[:], offs)
        load_scales([nc.scalar, nc.scalar, nc.sync, nc.sync], k_plane, keys_scales)
        for c, words in enumerate(k_words):
            nc.sync.dma_start(out=words[:].bitcast(I32),
                              in_=keys_words[0, :, 2 * c * BANK:2 * (c + 1) * BANK].bitcast(I32))
        nc.sync.dma_start(l2[:], offs2)
        load_scales([nc.sync] * 4, n_plane, notes_scales)
        nc.sync.dma_start(out=n_words[:].bitcast(I32),
                          in_=notes_words[0].rearrange("p n t -> p (n t)").bitcast(I32))
        nc.sync.dma_start(out=u_words[:].bitcast(I32), in_=users_words[0].bitcast(I32))
        nc.sync.dma_start(l4[:], offs4)
        load_scales([nc.sync] * 4, u_plane, users_scales)
        nc.sync.dma_start(l3[:], offs3)
        nc.sync.dma_start(l5[:], offs5)
        nc.sync.dma_start(l6[:], offs6)

        q_bf = keep.tile([P, Q, PACK], BF16, align_bytes=64)
        nc.vector.tensor_copy(out=q_bf[:].rearrange("p (c i) j -> p c j i", i=4),
                              in_=q_raw[:].rearrange("p j (c i) -> p c j i", i=4))
        q_codes = keep.tile([P, Q], U32, align_bytes=64)
        q_plane = keep.tile([P, Q], U8, align_bytes=64)
        nc.vector.quantize_mx(out=q_codes[:].bitcast(FP8X4), scales=q_plane[:],
                              in_=q_bf[:].rearrange("p q j -> p (q j)"))

        def scores(name, words, plane, width):
            bank = psum.tile([P, width], F32, name=name)
            nc.tensor.matmul_mx(out=bank[:], lhsT=q_codes[:].bitcast(FP8X4), lhsT_scale=q_plane[:],
                                rhs=words, rhs_scale=plane, start=True, stop=True)
            return bank

        a = keep.tile([P, T], F32, tag="a_then_tail")
        chunks = T // A_CHUNK
        a_max = keep.tile([P, chunks], F32, tag="max_then_f2")
        for c in range(chunks):
            c0, c1 = c * A_CHUNK, (c + 1) * A_CHUNK
            bank = scores("a%d" % c, k_words[c0 // BANK][:, 2 * (c0 % BANK):2 * (c0 % BANK + A_CHUNK)].bitcast(FP4X4), k_plane[:, c0:c1], A_CHUNK)
            nc.vector.tensor_scalar(out=a[:, c0:c1], in0=bank[:], scalar1=1.0, scalar2=None,
                                    op0=ALU.mult, op1=ALU.max, accum_out=a_max[:, c:c + 1])
        neg_ta = keep.tile([P, 1], F32, tag="bias_then_b")
        nc.vector.tensor_reduce(out=neg_ta[:], in_=a_max[:], axis=mybir.AxisListType.X, op=ALU.max, negate=True)

        f2 = keep.tile([P, U], F32, tag="max_then_f2")
        nc.vector.memset(f2[:], 0.0)
        for h in range(2):
            e1 = keep.tile([P, HALF], F32, name="e1_%d" % h)
            nc.scalar.activation(out=e1[:], in_=a[:].indirect(half(l1, h)), func=ACT.Exp, bias=neg_ta[:])
            nc.vector.tensor_tensor(out=f1[:].indirect(half(l2, h)), in0=e1[:], in1=fours[:], op=ALU.mult)

        def add_split(total, scattered, banks, tail):
            nc.gpsimd.tensor_tensor(out=total[:, SPLIT:], in0=scattered[:, SPLIT:], in1=tail, op=ALU.add)
            nc.vector.tensor_tensor(out=total[:, 0:BANK], in0=scattered[:, 0:BANK], in1=banks[0][:], op=ALU.add)
            nc.vector.tensor_tensor(out=total[:, BANK:SPLIT], in0=scattered[:, BANK:SPLIT],
                                    in1=banks[1][:, 0:SPLIT - BANK], op=ALU.add)

        b = keep.tile([P, U], F32, tag="bias_then_b")
        b_banks = []
        for c in range(U // BANK):
            c0, c1 = c * BANK, (c + 1) * BANK
            bank = scores("b%d" % c, n_words[:, c0:c1].bitcast(FP8X4), n_plane[:, c0:c1], BANK)
            nc.scalar.copy(out=b[:, c0:c1], in_=bank[:])
            b_banks.append(bank)
        neg_b = keep.tile([P, I], F32)
        nc.scalar.activation(out=neg_b[:], in_=b[:].indirect(l4[:]), func=ACT.Copy, scale=-1.0)

        cc = keep.tile([P, X], F32)
        c_banks = [scores("c%d" % c, u_words[:, 2 * c * BANK:2 * (c + 1) * BANK].bitcast(FP4X4),
                          u_plane[:, c * BANK:(c + 1) * BANK], BANK) for c in range(X // BANK)]
        c_tail = keep.tile([P, X - SPLIT], F32, tag="a_then_tail")
        nc.scalar.copy(out=c_tail[:], in_=c_banks[1][:, SPLIT - BANK:])

        add_split(cc, f1, c_banks, c_tail[:])

        picked = keep.tile([P, I], F32)
        nc.vector.tensor_copy(out=picked[:, 0:HALF], in_=cc[:].indirect(half(l3, 0)))
        nc.scalar.activation(out=picked[:, HALF:I], in_=cc[:].indirect(half(l3, 1)), func=ACT.Copy)
        nc.vector.tensor_tensor(out=f2[:].indirect(l5[:]), in0=picked[:], in1=neg_b[:], op=ALU.add)

        bb = keep.tile([P, U], F32)
        add_split(bb, f2, b_banks, b[:, SPLIT:])
        y = keep.tile([P, I], F32)
        nc.vector.tensor_copy(out=y[:, 0:HALF], in_=bb[:].indirect(half(l6, 0)))
        nc.scalar.activation(out=y[:, HALF:I], in_=bb[:].indirect(half(l6, 1)), func=ACT.Copy)
        nc.sync.dma_start(out=out, in_=y[:])
